import numpy as np
CORES = [0,8,16,24,32,40,48,56,64,72,80,88,96,104,112,120]
N = 16
ROOT = 11
def setup_inputs(rng):
    return {"x": rng.standard_normal((N, 128, 256), dtype=np.float32)}
def reference(x):
    y = np.full(x.shape, np.nan, x.dtype)
    y[ROOT] = x.sum(axis=0, dtype=np.float64).astype(x.dtype)
    return {"y": y}

@@ -1,0 +1,68 @@
+from concourse.bass import DstId, RemoteDMATransfer
+
+ROOT_RANK = 11
+NS = 8
+W = 32
+FOLDER = 2
+
+SCRATCH = {
+    "xs": ("dram", [NS, 128, W], "float32"),
+    "land": ("dram", [NS, 128, W], "float32"),
+    "part": ("dram", [2, 128, W], "float32"),
+    "res": ("dram", [NS, 128, W], "float32"),
+}
+SEMAPHORES = ["loaded", "arr", "sent", "fin", "stored"]
+
+
+def combiner(p, rootp):
+    base = (2 * p + 1) * 8
+    if p == rootp:
+        return base + 1
+    return base + (4 if p % 2 == 0 else 3)
+
+
+def rank_program(g, core, T, topo):
+    root = T.cores[ROOT_RANK]
+    rootp = topo.chip(root) // 2
+    chip = topo.chip(core)
+    k = core % 8
+    p = chip // 2
+    odd = chip & 1
+
+    def did(c):
+        rid, pid, se = topo.addr(c)
+        return DstId(rid=rid, pnc=pid)
+
+    if k == 0:
+        g.sync.dma_start(T.xs[:], T.x[:]).then_inc(T.sem.loaded, 16)
+        g.wait_ge(T.sem.loaded, 16)
+        trs = []
+        bit = 0
+        for q in range(NS):
+            if q == p:
+                m = 0x80
+            else:
+                m = 1 << bit
+                bit += 1
+            trs.append(RemoteDMATransfer(dst_ids=[did((2 * q + odd) * 8 + FOLDER)], dma_engine_mask=m,
+                                         remote_sem=T.sem.arr, src=T.xs[q], dst=T.land[p]))
+        g.remote_dma_fused(trs, local_sem=T.sem.sent)
+        if core == root:
+            g.sync.wait_ge(T.sem.fin, 7 * 8 + 16)
+            g.sync.dma_start(T.y[:], T.res[:]).then_inc(T.sem.stored, 16)
+            g.wait_ge(T.sem.stored, 16)
+        g.wait_ge(T.sem.sent, 8)
+    elif k == FOLDER:
+        g.wait_ge(T.sem.arr, 8)
+        n = 16 if odd else 8
+        g.remote_dma_fused([RemoteDMATransfer(dst_ids=[did(combiner(p, rootp))], dma_engine_mask=(1 << n) - 1,
+                                              remote_sem=T.sem.arr, srcs=[T.land[q] for q in range(NS)],
+                                              dsts=[T.part[odd]], alu_op=1)], local_sem=T.sem.sent)
+        g.wait_ge(T.sem.sent, n)
+    elif odd and core == combiner(p, rootp):
+        g.wait_ge(T.sem.arr, 16 + 8)
+        n = 16 if p == rootp else 8
+        g.remote_dma_fused([RemoteDMATransfer(dst_ids=[did(root)], dma_engine_mask=(1 << n) - 1,
+                                              remote_sem=T.sem.fin, srcs=[T.part[0], T.part[1]],
+                                              dsts=[T.res[p]], alu_op=1)], local_sem=T.sem.sent)
+        g.wait_ge(T.sem.sent, n)

@@ -2,23 +2,18 @@ from concourse.bass import DstId, RemoteDMATransfer
 
 ROOT_RANK = 11
 NS = 8
-W = 32
-FOLDER = 2
+C = 2
+W = 32 // C
+FOLDERS = [2, 3, 6, 7]
+COMBINERS = {1: [3, 4], 2: [1, 4], 4: [1, 4, 0, 5]}[C]
 
 SCRATCH = {
-    "xs": ("dram", [NS, 128, W], "float32"),
+    "xs": ("dram", [NS * C, 128, W], "float32"),
     "land": ("dram", [NS, 128, W], "float32"),
     "part": ("dram", [2, 128, W], "float32"),
-    "res": ("dram", [NS, 128, W], "float32"),
+    "res": ("dram", [NS * C, 128, W], "float32"),
 }
-SEMAPHORES = ["loaded", "arr", "sent", "fin", "stored"]
-
-
-def combiner(p, rootp):
-    base = (2 * p + 1) * 8
-    if p == rootp:
-        return base + 1
-    return base + (4 if p % 2 == 0 else 3)
+SEMAPHORES = ["arr", "sent", "stored"] + ["ld%d" % c for c in range(C)] + ["fin%d" % c for c in range(C)]
 
 
 def rank_program(g, core, T, topo):
@@ -28,41 +23,60 @@ def rank_program(g, core, T, topo):
     k = core % 8
     p = chip // 2
     odd = chip & 1
+    R = 128 // C
 
     def did(c):
         rid, pid, se = topo.addr(c)
         return DstId(rid=rid, pnc=pid)
 
+    def combiner(c):
+        if p == rootp:
+            return (2 * p + 1) * 8 + FOLDERS[c]
+        return (2 * p + 1) * 8 + COMBINERS[(c + p) % len(COMBINERS)]
+
+    def fold(srcs, dst_core, dst, sem):
+        n = 16 if topo.chip(dst_core) == chip else 8
+        g.remote_dma_fused([RemoteDMATransfer(dst_ids=[did(dst_core)], dma_engine_mask=(1 << n) - 1, remote_sem=sem,
+                                              srcs=srcs, dsts=[dst], alu_op=1)], local_sem=T.sem.sent)
+        return n
+
+    sent = 0
     if k == 0:
-        g.sync.dma_start(T.xs[:], T.x[:]).then_inc(T.sem.loaded, 16)
-        g.wait_ge(T.sem.loaded, 16)
-        trs = []
-        bit = 0
-        for q in range(NS):
-            if q == p:
-                m = 0x80
-            else:
-                m = 1 << bit
-                bit += 1
-            trs.append(RemoteDMATransfer(dst_ids=[did((2 * q + odd) * 8 + FOLDER)], dma_engine_mask=m,
-                                         remote_sem=T.sem.arr, src=T.xs[q], dst=T.land[p]))
-        g.remote_dma_fused(trs, local_sem=T.sem.sent)
+        queues = [g.sync, g.scalar]
+        for c in range(C):
+            queues[c % 2].dma_start(T.xs[c * NS:(c + 1) * NS], T.x[c * R:(c + 1) * R, :]).then_inc(T.sem["ld%d" % c], 16)
+        for c in range(C):
+            g.wait_ge(T.sem["ld%d" % c], 16)
+            trs = []
+            bit = 0
+            for q in range(NS):
+                if q == p:
+                    m = 0x80
+                else:
+                    m = 1 << bit
+                    bit += 1
+                trs.append(RemoteDMATransfer(dst_ids=[did((2 * q + odd) * 8 + FOLDERS[c])], dma_engine_mask=m,
+                                             remote_sem=T.sem.arr, src=T.xs[c * NS + q], dst=T.land[p]))
+            g.remote_dma_fused(trs, local_sem=T.sem.sent)
+            sent += 8
         if core == root:
-            g.sync.wait_ge(T.sem.fin, 7 * 8 + 16)
-            g.sync.dma_start(T.y[:], T.res[:]).then_inc(T.sem.stored, 16)
-            g.wait_ge(T.sem.stored, 16)
-        g.wait_ge(T.sem.sent, 8)
-    elif k == FOLDER:
-        g.wait_ge(T.sem.arr, 8)
-        n = 16 if odd else 8
-        g.remote_dma_fused([RemoteDMATransfer(dst_ids=[did(combiner(p, rootp))], dma_engine_mask=(1 << n) - 1,
-                                              remote_sem=T.sem.arr, srcs=[T.land[q] for q in range(NS)],
-                                              dsts=[T.part[odd]], alu_op=1)], local_sem=T.sem.sent)
-        g.wait_ge(T.sem.sent, n)
-    elif odd and core == combiner(p, rootp):
-        g.wait_ge(T.sem.arr, 16 + 8)
-        n = 16 if p == rootp else 8
-        g.remote_dma_fused([RemoteDMATransfer(dst_ids=[did(root)], dma_engine_mask=(1 << n) - 1,
-                                              remote_sem=T.sem.fin, srcs=[T.part[0], T.part[1]],
-                                              dsts=[T.res[p]], alu_op=1)], local_sem=T.sem.sent)
-        g.wait_ge(T.sem.sent, n)
+            for c in range(C):
+                queues[c % 2].wait_ge(T.sem["fin%d" % c], 7 * 8 + 16)
+                queues[c % 2].dma_start(T.y[c * R:(c + 1) * R, :], T.res[c * NS:(c + 1) * NS]).then_inc(T.sem.stored, 16)
+            g.wait_ge(T.sem.stored, 16 * C)
+    if k in FOLDERS[:C]:
+        c = FOLDERS.index(k)
+        srcs = [T.land[q] for q in range(NS)]
+        if odd and p == rootp:
+            g.wait_ge(T.sem.arr, 8 + 8)
+            sent += fold(srcs + [T.part[0]], root, T.res[c * NS + p], T.sem["fin%d" % c])
+        else:
+            g.wait_ge(T.sem.arr, 8)
+            sent += fold(srcs, combiner(c), T.part[odd], T.sem.arr)
+    if odd and p != rootp:
+        for c in range(C):
+            if core == combiner(c):
+                g.wait_ge(T.sem.arr, 16 + 8)
+                sent += fold([T.part[0], T.part[1]], root, T.res[c * NS + p], T.sem["fin%d" % c])
+    if sent:
+        g.wait_ge(T.sem.sent, sent)

@@ -2,17 +2,18 @@ from concourse.bass import DstId, RemoteDMATransfer
 
 ROOT_RANK = 11
 NS = 8
+WS = [20, 12]
 C = 2
-W = 32 // C
-FOLDERS = [2, 3, 6, 7]
-COMBINERS = {1: [3, 4], 2: [1, 4], 4: [1, 4, 0, 5]}[C]
+ROW0 = [0, 80, 128]
+FOLDERS = [2, 3]
+COMBINERS = [1, 4]
 
-SCRATCH = {
-    "xs": ("dram", [NS * C, 128, W], "float32"),
-    "land": ("dram", [NS, 128, W], "float32"),
-    "part": ("dram", [2, 128, W], "float32"),
-    "res": ("dram", [NS * C, 128, W], "float32"),
-}
+SCRATCH = {}
+for ci in range(C):
+    SCRATCH["xs%d" % ci] = ("dram", [NS, 128, WS[ci]], "float32")
+    SCRATCH["land%d" % ci] = ("dram", [NS, 128, WS[ci]], "float32")
+    SCRATCH["part%d" % ci] = ("dram", [2, 128, WS[ci]], "float32")
+    SCRATCH["res%d" % ci] = ("dram", [NS, 128, WS[ci]], "float32")
 SEMAPHORES = ["arr", "sent", "stored"] + ["ld%d" % c for c in range(C)] + ["fin%d" % c for c in range(C)]
 
 
@@ -23,7 +24,6 @@ def rank_program(g, core, T, topo):
     k = core % 8
     p = chip // 2
     odd = chip & 1
-    R = 128 // C
 
     def did(c):
         rid, pid, se = topo.addr(c)
@@ -32,7 +32,7 @@ def rank_program(g, core, T, topo):
     def combiner(c):
         if p == rootp:
             return (2 * p + 1) * 8 + FOLDERS[c]
-        return (2 * p + 1) * 8 + COMBINERS[(c + p) % len(COMBINERS)]
+        return (2 * p + 1) * 8 + COMBINERS[(c + p) % 2]
 
     def fold(srcs, dst_core, dst, sem):
         n = 16 if topo.chip(dst_core) == chip else 8
@@ -44,7 +44,7 @@ def rank_program(g, core, T, topo):
     if k == 0:
         queues = [g.sync, g.scalar]
         for c in range(C):
-            queues[c % 2].dma_start(T.xs[c * NS:(c + 1) * NS], T.x[c * R:(c + 1) * R, :]).then_inc(T.sem["ld%d" % c], 16)
+            queues[c].dma_start(T["xs%d" % c][:], T.x[ROW0[c]:ROW0[c + 1], :]).then_inc(T.sem["ld%d" % c], 16)
         for c in range(C):
             g.wait_ge(T.sem["ld%d" % c], 16)
             trs = []
@@ -56,27 +56,27 @@ def rank_program(g, core, T, topo):
                     m = 1 << bit
                     bit += 1
                 trs.append(RemoteDMATransfer(dst_ids=[did((2 * q + odd) * 8 + FOLDERS[c])], dma_engine_mask=m,
-                                             remote_sem=T.sem.arr, src=T.xs[c * NS + q], dst=T.land[p]))
+                                             remote_sem=T.sem.arr, src=T["xs%d" % c][q], dst=T["land%d" % c][p]))
             g.remote_dma_fused(trs, local_sem=T.sem.sent)
             sent += 8
         if core == root:
             for c in range(C):
-                queues[c % 2].wait_ge(T.sem["fin%d" % c], 7 * 8 + 16)
-                queues[c % 2].dma_start(T.y[c * R:(c + 1) * R, :], T.res[c * NS:(c + 1) * NS]).then_inc(T.sem.stored, 16)
+                queues[c].wait_ge(T.sem["fin%d" % c], 7 * 8 + 16)
+                queues[c].dma_start(T.y[ROW0[c]:ROW0[c + 1], :], T["res%d" % c][:]).then_inc(T.sem.stored, 16)
             g.wait_ge(T.sem.stored, 16 * C)
-    if k in FOLDERS[:C]:
+    if k in FOLDERS:
         c = FOLDERS.index(k)
-        srcs = [T.land[q] for q in range(NS)]
+        srcs = [T["land%d" % c][q] for q in range(NS)]
         if odd and p == rootp:
             g.wait_ge(T.sem.arr, 8 + 8)
-            sent += fold(srcs + [T.part[0]], root, T.res[c * NS + p], T.sem["fin%d" % c])
+            sent += fold(srcs + [T["part%d" % c][0]], root, T["res%d" % c][p], T.sem["fin%d" % c])
         else:
             g.wait_ge(T.sem.arr, 8)
-            sent += fold(srcs, combiner(c), T.part[odd], T.sem.arr)
+            sent += fold(srcs, combiner(c), T["part%d" % c][odd], T.sem.arr)
     if odd and p != rootp:
         for c in range(C):
             if core == combiner(c):
                 g.wait_ge(T.sem.arr, 16 + 8)
-                sent += fold([T.part[0], T.part[1]], root, T.res[c * NS + p], T.sem["fin%d" % c])
+                sent += fold([T["part%d" % c][0], T["part%d" % c][1]], root, T["res%d" % c][p], T.sem["fin%d" % c])
     if sent:
         g.wait_ge(T.sem.sent, sent)

from concourse.bass import DstId, RemoteDMATransfer

ROOT_RANK = 11
NS = 8
WS = [20, 12]
C = 2
ROW0 = [0, 80, 128]
FOLDERS = [2, 3]
COMBINERS = [1, 4]

SCRATCH = {}
for ci in range(C):
    SCRATCH["xs%d" % ci] = ("dram", [NS, 128, WS[ci]], "float32")
    SCRATCH["land%d" % ci] = ("dram", [NS, 128, WS[ci]], "float32")
    SCRATCH["part%d" % ci] = ("dram", [2, 128, WS[ci]], "float32")
    SCRATCH["res%d" % ci] = ("dram", [NS, 128, WS[ci]], "float32")
SEMAPHORES = ["arr", "sent", "stored"] + ["ld%d" % c for c in range(C)] + ["fin%d" % c for c in range(C)]


def rank_program(g, core, T, topo):
    root = T.cores[ROOT_RANK]
    rootp = topo.chip(root) // 2
    chip = topo.chip(core)
    k = core % 8
    p = chip // 2
    odd = chip & 1

    def did(c):
        rid, pid, se = topo.addr(c)
        return DstId(rid=rid, pnc=pid)

    def combiner(c):
        if p == rootp:
            return (2 * p + 1) * 8 + FOLDERS[c]
        return (2 * p + 1) * 8 + COMBINERS[(c + p) % 2]

    def fold(srcs, dst_core, dst, sem):
        n = 16 if topo.chip(dst_core) == chip else 8
        g.remote_dma_fused([RemoteDMATransfer(dst_ids=[did(dst_core)], dma_engine_mask=(1 << n) - 1, remote_sem=sem,
                                              srcs=srcs, dsts=[dst], alu_op=1)], local_sem=T.sem.sent)
        return n

    sent = 0
    if k == 0:
        queues = [g.sync, g.scalar]
        for c in range(C):
            queues[c].dma_start(T["xs%d" % c][:], T.x[ROW0[c]:ROW0[c + 1], :]).then_inc(T.sem["ld%d" % c], 16)
        for c in range(C):
            g.wait_ge(T.sem["ld%d" % c], 16)
            trs = []
            bit = 0
            for q in range(NS):
                if q == p:
                    m = 0x80
                else:
                    m = 1 << bit
                    bit += 1
                trs.append(RemoteDMATransfer(dst_ids=[did((2 * q + odd) * 8 + FOLDERS[c])], dma_engine_mask=m,
                                             remote_sem=T.sem.arr, src=T["xs%d" % c][q], dst=T["land%d" % c][p]))
            g.remote_dma_fused(trs, local_sem=T.sem.sent)
            sent += 8
        if core == root:
            for c in range(C):
                queues[c].wait_ge(T.sem["fin%d" % c], 7 * 8 + 16)
                queues[c].dma_start(T.y[ROW0[c]:ROW0[c + 1], :], T["res%d" % c][:]).then_inc(T.sem.stored, 16)
            g.wait_ge(T.sem.stored, 16 * C)
    if k in FOLDERS:
        c = FOLDERS.index(k)
        srcs = [T["land%d" % c][q] for q in range(NS)]
        if odd and p == rootp:
            g.wait_ge(T.sem.arr, 8 + 8)
            sent += fold(srcs + [T["part%d" % c][0]], root, T["res%d" % c][p], T.sem["fin%d" % c])
        else:
            g.wait_ge(T.sem.arr, 8)
            sent += fold(srcs, combiner(c), T["part%d" % c][odd], T.sem.arr)
    if odd and p != rootp:
        for c in range(C):
            if core == combiner(c):
                g.wait_ge(T.sem.arr, 16 + 8)
                sent += fold([T["part%d" % c][0], T["part%d" % c][1]], root, T["res%d" % c][p], T.sem["fin%d" % c])
    if sent:
        g.wait_ge(T.sem.sent, sent)
